import numpy as np
import ml_dtypes


def mxq(x, axis, fmt="e4m3"):
    dtype, down = {"e4m3": (ml_dtypes.float8_e4m3fn, 7), "e5m2": (ml_dtypes.float8_e5m2, 14)}[fmt]
    v = np.moveaxis(np.asarray(x, np.float32).astype(ml_dtypes.bfloat16).astype(np.float64), axis, -1)
    blocks = v.reshape(v.shape[:-1] + (-1, 32))
    amax = np.abs(blocks).max(-1, keepdims=True)
    byte = np.maximum(np.where(amax > 0, np.frexp(amax)[1] - 1 + 127, 0) - down, 1)
    scale = np.exp2(byte - 127.0)
    codes = (blocks / scale).astype(np.float32).astype(dtype).astype(np.float64)
    return np.moveaxis((codes * scale).reshape(v.shape), -1, axis)


WIDE = False


def mx_kscale(k):
    if not WIDE:
        return np.ones(k)
    levels = np.array([10, -10, 5, -5, 0])
    if k % 512:
        return np.exp2(np.random.permutation(np.resize(levels, k // 32))).repeat(32)
    a = np.empty((k // 512, 16))
    for p in range(k // 512):
        a[p, :8] = np.random.permutation(np.resize(levels, 8))
        for g in range(8):
            far = levels[np.abs(levels - a[p, g]) >= 10]
            a[p, g + 8] = far[np.random.randint(len(far))]
    return np.exp2(a.ravel()).repeat(32)


def f64(x):
    return np.asarray(x).astype(np.float64)


def striped(idx):
    return np.tile(idx.reshape(-1, 16).T, (8, 1)).astype(np.uint16)


def unstriped(offs):
    return offs[:16].T.reshape(-1).astype(np.int64)


def pack_weight(w):
    k, n = w.shape
    w = f64(np.asarray(w, np.float32).astype(ml_dtypes.bfloat16)).reshape(k // 32, 32, n)
    amax = np.abs(w).max(1)
    byte = np.clip(np.where(amax > 0, np.frexp(amax)[1] - 1 + 127 - 7, 1), 1, 254)
    scaled = (w * np.exp2(127.0 - byte)[:, None, :]).reshape(k, n).astype(np.float32)
    words = np.ascontiguousarray(scaled.reshape(k // 512, 128, 4, n).transpose(0, 1, 3, 2)).astype(ml_dtypes.float8_e4m3fn).view(np.uint8)
    return words, np.ascontiguousarray(byte.astype(np.uint8).reshape(k // 512, 16, n))


def unpack_weight(words, scales):
    g, p, n, _ = words.shape
    vals = np.ascontiguousarray(words).view(ml_dtypes.float8_e4m3fn).astype(np.float64) * np.repeat(np.exp2(scales.astype(np.float64) - 127.0), 8, axis=1)[..., None]
    return vals.transpose(0, 1, 3, 2).reshape(g * 512, n)


K, T, S, N, W = 512, 2048, 256, 512, 128


def setup_inputs():
    n = np.random.standard_normal
    s = mx_kscale(K)[:, None]
    packed_xT = pack_weight(n((K, T)) * s)
    perm = np.random.permutation(S)
    return {
        "x_words": packed_xT[0],
        "x_scales": packed_xT[1],
        "w1": (n((K, N)) / np.sqrt(2 * K) / s).astype(np.float32),
        "w2": (n((K, N)) / np.sqrt(2 * K) / s).astype(np.float32),
        "offs": striped(np.random.permutation(T)[:S]),
        "two": striped(np.random.permutation(T)[:S]),
        "n1": striped(perm[:W]),
        "n2": striped(perm[W:]),
    }


def reference(x_words, x_scales, w1, w2, offs, two, n1, n2):
    xq = unpack_weight(x_words, x_scales)[:, unstriped(offs)]
    x_two = unpack_weight(x_words, x_scales)[:, unstriped(two)]
    h = mxq(f64(w1), 0, "e4m3").T @ xq + mxq(f64(w2), 0, "e4m3").T @ x_two
    pa = h[:, unstriped(n1)]
    pb = h[:, unstriped(n2)]
    rb = pa - pb
    ra = 0.75 * (pa + pb)
    ds = np.zeros((N, S))
    ds[:, unstriped(n1)] = ra
    out = ds.copy()
    out[:, unstriped(n2)] = rb
    return out

@@ -1,0 +1,132 @@
+from contextlib import ExitStack
+
+import concourse.mybir as mybir
+
+K, T, S, N, W = 512, 2048, 256, 512, 128
+FLOPS = 2 * 2 * K * N * S
+
+F32 = mybir.dt.float32
+BF16 = mybir.dt.bfloat16
+I32 = mybir.dt.int32
+U32 = mybir.dt.uint32
+U16 = mybir.dt.uint16
+U8 = mybir.dt.uint8
+FP8X4 = mybir.dt.float8_e4m3fn_x4
+COPY = mybir.ActivationFunctionType.Copy
+ALU = mybir.AluOpType
+
+P = 128
+PACK = 4
+BLOCKS = N // P
+
+
+def tile_picked_otthaar_none_p_kernel(tc, x_words, x_scales, w1, w2, offs, two, n1, n2, out):
+    nc = tc.nc
+    with ExitStack() as ctx:
+        keep = ctx.enter_context(tc.tile_pool(name="keep", bufs=1))
+        psum = ctx.enter_context(tc.psum_pool(name="psum", bufs=1))
+
+        def load_list(src, entries, name):
+            t = keep.tile([P, entries // 16], U16, name=name)
+            nc.sync.dma_start(t[:], src)
+            return t
+
+        def load_w(w, i, b):
+            t = keep.tile([P, PACK, P], F32, name="raw%d_%d" % (i, b))
+            nc.sync.dma_start(t[:], w.rearrange("(p j) m -> p j m", j=PACK)[:, :, b * P:(b + 1) * P])
+            return t
+
+        scale_table = keep.tile([P, T], U8, name="scale_table")
+        nc.vector.memset(scale_table[:].bitcast(I32), 0)
+        for q in range(4):
+            nc.sync.dma_start(scale_table[32 * q:32 * q + 4, :].bitcast(I32),
+                                x_scales[0, 4 * q:4 * q + 4, :].bitcast(I32))
+
+        raw = {}
+        raw[0, 0] = load_w(w1, 0, 0)
+        l_offs = load_list(offs, S, "l_offs")
+        l_two = load_list(two, S, "l_two")
+        word_table = keep.tile([P, T], U32, name="word_table")
+        nc.sync.dma_start(word_table[:].bitcast(I32), x_words[0].rearrange("p n t -> p (n t)").bitcast(I32))
+        raw[1, 0] = load_w(w2, 1, 0)
+        raw[0, 1] = load_w(w1, 0, 1)
+        l_n1 = load_list(n1, W, "l_n1")
+        l_n2 = load_list(n2, W, "l_n2")
+        raw[1, 1] = load_w(w2, 1, 1)
+        for b in range(2, BLOCKS):
+            raw[0, b] = load_w(w1, 0, b)
+            raw[1, b] = load_w(w2, 1, b)
+
+        rounded = [keep.tile([P, 2, P, PACK], BF16, name="rounded%d" % b, tag="rounded%d" % b, align_bytes=64) for b in range(BLOCKS)]
+        codes = [keep.tile([P, 2, P], U32, name="codes%d" % b, tag="codes%d" % b, align_bytes=64) for b in range(BLOCKS)]
+        scales = [keep.tile([P, 2, P], U8, name="scales%d" % b, align_bytes=64) for b in range(BLOCKS)]
+
+        def cast(i, b, on_scalar):
+            dst = rounded[b][:, i].rearrange("p (c e) j -> p c j e", e=4)
+            src = raw[i, b][:].rearrange("p j (c e) -> p c j e", e=4)
+            if on_scalar:
+                nc.scalar.activation(dst, src, COPY)
+            else:
+                nc.vector.tensor_copy(dst, src)
+
+        def quantize(b, lo, hi):
+            nc.vector.quantize_mx(
+                out=codes[b][:, lo:hi].rearrange("p i m -> p (i m)").bitcast(FP8X4),
+                scales=scales[b][:, lo:hi].rearrange("p i m -> p (i m)"),
+                in_=rounded[b][:, lo:hi].rearrange("p i m j -> p (i m j)"))
+
+        picked_scales = []
+        picked_words = []
+        for i, lst in enumerate((l_offs, l_two)):
+            t = keep.tile([P, S], U8, name="picked_scales%d" % i, align_bytes=64)
+            nc.vector.tensor_copy(t[:], scale_table[:].indirect(lst[:]))
+            picked_scales.append(t)
+        cast(0, 0, True)
+        quantize(0, 0, 1)
+        for i, lst in enumerate((l_offs, l_two)):
+            t = keep.tile([P, S], U32, name="picked_words%d" % i, align_bytes=64)
+            nc.vector.tensor_copy(t[:], word_table[:].indirect(lst[:]))
+            picked_words.append(t)
+        cast(1, 0, True)
+        quantize(0, 1, 2)
+
+        h = [keep.tile([P, S], F32, name="h%d" % b) for b in range(BLOCKS)]
+        pa = [keep.tile([P, W], F32, name="pa%d" % b) for b in range(BLOCKS)]
+        pb = [keep.tile([P, W], F32, name="pb%d" % b) for b in range(BLOCKS)]
+        res = [keep.tile([P, S], F32, name="res%d" % b) for b in range(BLOCKS)]
+
+        def product(b):
+            acc = psum.tile([P, S], F32, name="acc%d" % b)
+            for i in range(2):
+                nc.tensor.matmul_mx(out=acc[:], lhsT=codes[b][:, i].bitcast(FP8X4), lhsT_scale=scales[b][:, i],
+                                    rhs=picked_words[i][:].bitcast(FP8X4), rhs_scale=picked_scales[i][:],
+                                    start=(i == 0), stop=(i == 1))
+            nc.vector.tensor_copy(h[b][:], acc[:])
+
+        def fetch(b):
+            nc.scalar.activation(pa[b][:], h[b][:].indirect(l_n1[:]), COPY)
+            nc.scalar.activation(pb[b][:], h[b][:].indirect(l_n2[:]), COPY)
+
+        def combine(b, op, name, tag):
+            t = keep.tile([P, W], F32, name="%s%d" % (name, b), tag="%s%d" % (tag, b + 1), align_bytes=64)
+            nc.vector.tensor_tensor(t[:], pa[b][:], pb[b][:], op)
+            return t
+
+        def prepare(b):
+            cast(0, b, False)
+            cast(1, b, False)
+            quantize(b, 0, 2)
+
+        product(0)
+        fetch(0)
+        for b in range(BLOCKS):
+            if b + 1 < BLOCKS:
+                prepare(b + 1)
+            ra = combine(b, ALU.add, "ra", "rounded")
+            nc.scalar.activation(res[b][:].indirect(l_n1[:]), ra[:], COPY, scale=0.75)
+            if b + 1 < BLOCKS:
+                product(b + 1)
+                fetch(b + 1)
+            rb = combine(b, ALU.subtract, "rb", "codes")
+            nc.scalar.activation(res[b][:].indirect(l_n2[:]), rb[:], COPY)
+            nc.sync.dma_start(out[b * P:(b + 1) * P, :], res[b][:])

@@ -48,7 +48,11 @@ def tile_picked_otthaar_none_p_kernel(tc, x_words, x_scales, w1, w2, offs, two, 
         l_two = load_list(two, S, "l_two")
         word_table = keep.tile([P, T], U32, name="word_table")
         nc.sync.dma_start(word_table[:].bitcast(I32), x_words[0].rearrange("p n t -> p (n t)").bitcast(I32))
-        raw[1, 0] = load_w(w2, 1, 0)
+        last_rows = []
+        for u in range(2):
+            t = keep.tile([P, 2, P], F32, name="last_rows%d" % u)
+            nc.sync.dma_start(t[:], w2.rearrange("(p j) m -> p j m", j=PACK)[:, 2 * u:2 * u + 2, 0:P])
+            last_rows.append(t)
         raw[0, 1] = load_w(w1, 0, 1)
         l_n1 = load_list(n1, W, "l_n1")
         l_n2 = load_list(n2, W, "l_n2")
@@ -57,9 +61,9 @@ def tile_picked_otthaar_none_p_kernel(tc, x_words, x_scales, w1, w2, offs, two, 
             raw[0, b] = load_w(w1, 0, b)
             raw[1, b] = load_w(w2, 1, b)
 
-        rounded = [keep.tile([P, 2, P, PACK], BF16, name="rounded%d" % b, tag="rounded%d" % b, align_bytes=64) for b in range(BLOCKS)]
+        rounded = {b: keep.tile([P, 2, P, PACK], BF16, name="rounded%d" % b, tag="rounded%d" % b, align_bytes=64) for b in range(2)}
         codes = [keep.tile([P, 2, P], U32, name="codes%d" % b, tag="codes%d" % b, align_bytes=64) for b in range(BLOCKS)]
-        scales = [keep.tile([P, 2, P], U8, name="scales%d" % b, align_bytes=64) for b in range(BLOCKS)]
+        scales = [keep.tile([P, 2, P], U8, name="scales%d" % b, tag="rounded%d" % (b + 1) if b in (1, 2) else "scales%d" % b, align_bytes=64) for b in range(BLOCKS)]
 
         def cast(i, b, on_scalar):
             dst = rounded[b][:, i].rearrange("p (c e) j -> p c j e", e=4)
@@ -87,7 +91,9 @@ def tile_picked_otthaar_none_p_kernel(tc, x_words, x_scales, w1, w2, offs, two, 
             t = keep.tile([P, S], U32, name="picked_words%d" % i, align_bytes=64)
             nc.vector.tensor_copy(t[:], word_table[:].indirect(lst[:]))
             picked_words.append(t)
-        cast(1, 0, True)
+        for u in range(2):
+            nc.scalar.activation(rounded[0][:, 1].rearrange("p (c e) j -> p c j e", e=4)[:, :, 2 * u:2 * u + 2, :],
+                                 last_rows[u][:].rearrange("p j (c e) -> p c j e", e=4), COPY)
         quantize(0, 1, 2)
 
         h = [keep.tile([P, S], F32, name="h%d" % b) for b in range(BLOCKS)]
@@ -113,13 +119,39 @@ def tile_picked_otthaar_none_p_kernel(tc, x_words, x_scales, w1, w2, offs, two, 
             return t
 
         def prepare(b):
-            cast(0, b, False)
-            cast(1, b, False)
-            quantize(b, 0, 2)
+            if b > 1:
+                rounded[b] = keep.tile([P, 2, P, PACK], BF16, name="rounded%d" % b, tag="rounded%d" % b, align_bytes=64)
+            for i in range(2):
+                cast(i, b, False)
+                quantize(b, i, i + 1)
 
-        product(0)
-        fetch(0)
-        for b in range(BLOCKS):
+        halves = [psum.tile([P, S // 2], F32, name="half%d" % u) for u in range(2)]
+        for i in range(2):
+            for u in range(2):
+                cols = slice(u * S // 2, (u + 1) * S // 2)
+                nc.tensor.matmul_mx(out=halves[u][:], lhsT=codes[0][:, i].bitcast(FP8X4), lhsT_scale=scales[0][:, i],
+                                    rhs=picked_words[i][:, cols].bitcast(FP8X4), rhs_scale=picked_scales[i][:, cols],
+                                    start=(i == 0), stop=(i == 1))
+        for u in range(2):
+            nc.scalar.activation(h[0][:, u * S // 2:(u + 1) * S // 2], halves[u][:], COPY)
+        H = W // 2
+        for u in range(2):
+            nc.scalar.activation(pa[0][:, u * H:(u + 1) * H], h[0][:].indirect(l_n1[:, 4 * u:4 * u + 4]), COPY)
+            nc.scalar.activation(pb[0][:, u * H:(u + 1) * H], h[0][:].indirect(l_n2[:, 4 * u:4 * u + 4]), COPY)
+        prepare(1)
+        ra_first = keep.tile([P, H], F32, name="ra_first", tag="rounded1", align_bytes=64)
+        nc.vector.tensor_tensor(ra_first[:], pa[0][:, 0:H], pb[0][:, 0:H], ALU.add)
+        nc.scalar.activation(res[0][:].indirect(l_n1[:, 0:4]), ra_first[:], COPY, scale=0.75)
+        product(1)
+        late = keep.tile([P, H + W], F32, name="late", tag="codes1", align_bytes=64)
+        nc.vector.tensor_tensor(late[:, 0:H], pa[0][:, H:W], pb[0][:, H:W], ALU.add)
+        nc.vector.tensor_tensor(late[:, H:H + W], pa[0][:], pb[0][:], ALU.subtract)
+        nc.scalar.activation(pa[1][:], h[1][:].indirect(l_n1[:]), COPY)
+        nc.scalar.activation(res[0][:].indirect(l_n1[:, 4:8]), late[:, 0:H], COPY, scale=0.75)
+        nc.scalar.activation(pb[1][:], h[1][:].indirect(l_n2[:]), COPY)
+        nc.scalar.activation(res[0][:].indirect(l_n2[:]), late[:, H:H + W], COPY)
+        nc.sync.dma_start(out[0:P, :], res[0][:])
+        for b in range(1, BLOCKS):
             if b + 1 < BLOCKS:
                 prepare(b + 1)
             ra = combine(b, ALU.add, "ra", "rounded")

@@ -38,9 +38,8 @@ def tile_picked_otthaar_none_p_kernel(tc, x_words, x_scales, w1, w2, offs, two, 
 
         scale_table = keep.tile([P, T], U8, name="scale_table")
         nc.vector.memset(scale_table[:].bitcast(I32), 0)
-        for q in range(4):
-            nc.sync.dma_start(scale_table[32 * q:32 * q + 4, :].bitcast(I32),
-                                x_scales[0, 4 * q:4 * q + 4, :].bitcast(I32))
+        for r in range(4):
+            nc.sync.dma_start(scale_table[r:P:32, :].bitcast(I32), x_scales[0, r:16:4, :].bitcast(I32))
 
         raw = {}
         raw[0, 0] = load_w(w1, 0, 0)

from contextlib import ExitStack

import concourse.mybir as mybir

K, T, S, N, W = 512, 2048, 256, 512, 128
FLOPS = 2 * 2 * K * N * S

F32 = mybir.dt.float32
BF16 = mybir.dt.bfloat16
I32 = mybir.dt.int32
U32 = mybir.dt.uint32
U16 = mybir.dt.uint16
U8 = mybir.dt.uint8
FP8X4 = mybir.dt.float8_e4m3fn_x4
COPY = mybir.ActivationFunctionType.Copy
ALU = mybir.AluOpType

P = 128
PACK = 4
BLOCKS = N // P


def tile_picked_otthaar_none_p_kernel(tc, x_words, x_scales, w1, w2, offs, two, n1, n2, out):
    nc = tc.nc
    with ExitStack() as ctx:
        keep = ctx.enter_context(tc.tile_pool(name="keep", bufs=1))
        psum = ctx.enter_context(tc.psum_pool(name="psum", bufs=1))

        def load_list(src, entries, name):
            t = keep.tile([P, entries // 16], U16, name=name)
            nc.sync.dma_start(t[:], src)
            return t

        def load_w(w, i, b):
            t = keep.tile([P, PACK, P], F32, name="raw%d_%d" % (i, b))
            nc.sync.dma_start(t[:], w.rearrange("(p j) m -> p j m", j=PACK)[:, :, b * P:(b + 1) * P])
            return t

        scale_table = keep.tile([P, T], U8, name="scale_table")
        nc.vector.memset(scale_table[:].bitcast(I32), 0)
        for r in range(4):
            nc.sync.dma_start(scale_table[r:P:32, :].bitcast(I32), x_scales[0, r:16:4, :].bitcast(I32))

        raw = {}
        raw[0, 0] = load_w(w1, 0, 0)
        l_offs = load_list(offs, S, "l_offs")
        l_two = load_list(two, S, "l_two")
        word_table = keep.tile([P, T], U32, name="word_table")
        nc.sync.dma_start(word_table[:].bitcast(I32), x_words[0].rearrange("p n t -> p (n t)").bitcast(I32))
        last_rows = []
        for u in range(2):
            t = keep.tile([P, 2, P], F32, name="last_rows%d" % u)
            nc.sync.dma_start(t[:], w2.rearrange("(p j) m -> p j m", j=PACK)[:, 2 * u:2 * u + 2, 0:P])
            last_rows.append(t)
        raw[0, 1] = load_w(w1, 0, 1)
        l_n1 = load_list(n1, W, "l_n1")
        l_n2 = load_list(n2, W, "l_n2")
        raw[1, 1] = load_w(w2, 1, 1)
        for b in range(2, BLOCKS):
            raw[0, b] = load_w(w1, 0, b)
            raw[1, b] = load_w(w2, 1, b)

        rounded = {b: keep.tile([P, 2, P, PACK], BF16, name="rounded%d" % b, tag="rounded%d" % b, align_bytes=64) for b in range(2)}
        codes = [keep.tile([P, 2, P], U32, name="codes%d" % b, tag="codes%d" % b, align_bytes=64) for b in range(BLOCKS)]
        scales = [keep.tile([P, 2, P], U8, name="scales%d" % b, tag="rounded%d" % (b + 1) if b in (1, 2) else "scales%d" % b, align_bytes=64) for b in range(BLOCKS)]

        def cast(i, b, on_scalar):
            dst = rounded[b][:, i].rearrange("p (c e) j -> p c j e", e=4)
            src = raw[i, b][:].rearrange("p j (c e) -> p c j e", e=4)
            if on_scalar:
                nc.scalar.activation(dst, src, COPY)
            else:
                nc.vector.tensor_copy(dst, src)

        def quantize(b, lo, hi):
            nc.vector.quantize_mx(
                out=codes[b][:, lo:hi].rearrange("p i m -> p (i m)").bitcast(FP8X4),
                scales=scales[b][:, lo:hi].rearrange("p i m -> p (i m)"),
                in_=rounded[b][:, lo:hi].rearrange("p i m j -> p (i m j)"))

        picked_scales = []
        picked_words = []
        for i, lst in enumerate((l_offs, l_two)):
            t = keep.tile([P, S], U8, name="picked_scales%d" % i, align_bytes=64)
            nc.vector.tensor_copy(t[:], scale_table[:].indirect(lst[:]))
            picked_scales.append(t)
        cast(0, 0, True)
        quantize(0, 0, 1)
        for i, lst in enumerate((l_offs, l_two)):
            t = keep.tile([P, S], U32, name="picked_words%d" % i, align_bytes=64)
            nc.vector.tensor_copy(t[:], word_table[:].indirect(lst[:]))
            picked_words.append(t)
        for u in range(2):
            nc.scalar.activation(rounded[0][:, 1].rearrange("p (c e) j -> p c j e", e=4)[:, :, 2 * u:2 * u + 2, :],
                                 last_rows[u][:].rearrange("p j (c e) -> p c j e", e=4), COPY)
        quantize(0, 1, 2)

        h = [keep.tile([P, S], F32, name="h%d" % b) for b in range(BLOCKS)]
        pa = [keep.tile([P, W], F32, name="pa%d" % b) for b in range(BLOCKS)]
        pb = [keep.tile([P, W], F32, name="pb%d" % b) for b in range(BLOCKS)]
        res = [keep.tile([P, S], F32, name="res%d" % b) for b in range(BLOCKS)]

        def product(b):
            acc = psum.tile([P, S], F32, name="acc%d" % b)
            for i in range(2):
                nc.tensor.matmul_mx(out=acc[:], lhsT=codes[b][:, i].bitcast(FP8X4), lhsT_scale=scales[b][:, i],
                                    rhs=picked_words[i][:].bitcast(FP8X4), rhs_scale=picked_scales[i][:],
                                    start=(i == 0), stop=(i == 1))
            nc.vector.tensor_copy(h[b][:], acc[:])

        def fetch(b):
            nc.scalar.activation(pa[b][:], h[b][:].indirect(l_n1[:]), COPY)
            nc.scalar.activation(pb[b][:], h[b][:].indirect(l_n2[:]), COPY)

        def combine(b, op, name, tag):
            t = keep.tile([P, W], F32, name="%s%d" % (name, b), tag="%s%d" % (tag, b + 1), align_bytes=64)
            nc.vector.tensor_tensor(t[:], pa[b][:], pb[b][:], op)
            return t

        def prepare(b):
            if b > 1:
                rounded[b] = keep.tile([P, 2, P, PACK], BF16, name="rounded%d" % b, tag="rounded%d" % b, align_bytes=64)
            for i in range(2):
                cast(i, b, False)
                quantize(b, i, i + 1)

        halves = [psum.tile([P, S // 2], F32, name="half%d" % u) for u in range(2)]
        for i in range(2):
            for u in range(2):
                cols = slice(u * S // 2, (u + 1) * S // 2)
                nc.tensor.matmul_mx(out=halves[u][:], lhsT=codes[0][:, i].bitcast(FP8X4), lhsT_scale=scales[0][:, i],
                                    rhs=picked_words[i][:, cols].bitcast(FP8X4), rhs_scale=picked_scales[i][:, cols],
                                    start=(i == 0), stop=(i == 1))
        for u in range(2):
            nc.scalar.activation(h[0][:, u * S // 2:(u + 1) * S // 2], halves[u][:], COPY)
        H = W // 2
        for u in range(2):
            nc.scalar.activation(pa[0][:, u * H:(u + 1) * H], h[0][:].indirect(l_n1[:, 4 * u:4 * u + 4]), COPY)
            nc.scalar.activation(pb[0][:, u * H:(u + 1) * H], h[0][:].indirect(l_n2[:, 4 * u:4 * u + 4]), COPY)
        prepare(1)
        ra_first = keep.tile([P, H], F32, name="ra_first", tag="rounded1", align_bytes=64)
        nc.vector.tensor_tensor(ra_first[:], pa[0][:, 0:H], pb[0][:, 0:H], ALU.add)
        nc.scalar.activation(res[0][:].indirect(l_n1[:, 0:4]), ra_first[:], COPY, scale=0.75)
        product(1)
        late = keep.tile([P, H + W], F32, name="late", tag="codes1", align_bytes=64)
        nc.vector.tensor_tensor(late[:, 0:H], pa[0][:, H:W], pb[0][:, H:W], ALU.add)
        nc.vector.tensor_tensor(late[:, H:H + W], pa[0][:], pb[0][:], ALU.subtract)
        nc.scalar.activation(pa[1][:], h[1][:].indirect(l_n1[:]), COPY)
        nc.scalar.activation(res[0][:].indirect(l_n1[:, 4:8]), late[:, 0:H], COPY, scale=0.75)
        nc.scalar.activation(pb[1][:], h[1][:].indirect(l_n2[:]), COPY)
        nc.scalar.activation(res[0][:].indirect(l_n2[:]), late[:, H:H + W], COPY)
        nc.sync.dma_start(out[0:P, :], res[0][:])
        for b in range(1, BLOCKS):
            if b + 1 < BLOCKS:
                prepare(b + 1)
            ra = combine(b, ALU.add, "ra", "rounded")
            nc.scalar.activation(res[b][:].indirect(l_n1[:]), ra[:], COPY, scale=0.75)
            if b + 1 < BLOCKS:
                product(b + 1)
                fetch(b + 1)
            rb = combine(b, ALU.subtract, "rb", "codes")
            nc.scalar.activation(res[b][:].indirect(l_n2[:]), rb[:], COPY)
            nc.sync.dma_start(out[b * P:(b + 1) * P, :], res[b][:])
